import numpy as np
import ml_dtypes

BF16 = ml_dtypes.bfloat16


def bf(x):
    return np.asarray(x, np.float32).astype(BF16)


def f32(x):
    return np.asarray(x, np.float32)


def f64(x):
    return np.asarray(x).astype(np.float64)


def striped(idx):
    return np.tile(idx.reshape(-1, 16).T, (8, 1))


S, K, M, N, D, V = 1024, 128, 512, 384, 4, 96


def setup_inputs():
    return {"table": bf(np.random.standard_normal((K, S))), "w": bf(np.random.standard_normal((K, M)) / np.sqrt(K)), "b": f32(0.5 * np.random.standard_normal((M, 1))), "offs": striped(np.random.permutation(np.tile(np.arange(S), 2))[:N])}


def reference(table, w, b, offs):
    idx = offs[:16].T.reshape(-1)
    x = f64(table)[:, idx]
    y = f64(w).T @ x
    z = np.tanh(y + f64(b))
    return z.reshape(M, V, D).max(axis=2)

@@ -1,0 +1,51 @@
+import concourse.mybir as mybir
+
+BF16, F32, U16 = mybir.dt.bfloat16, mybir.dt.float32, mybir.dt.uint16
+TANH = mybir.ActivationFunctionType.Tanh
+MAX = mybir.AluOpType.max
+X = mybir.AxisListType.X
+
+P = 128
+S = 1024
+M = 512
+N = 384
+D = 4
+V = N // D
+BLOCKS = M // P
+
+FLOPS = 2 * P * M * N
+
+
+def tile_gather_matmul_kernel(tc, table, w, b, offs, out):
+    nc = tc.nc
+    with (
+        tc.tile_pool(name="held", bufs=1) as held,
+        tc.tile_pool(name="work", bufs=2) as work,
+        tc.psum_pool(name="banks", bufs=BLOCKS) as banks,
+    ):
+        offsets = held.tile([P, N // 16], U16, name="offsets")
+        nc.sync.dma_start(offsets[:], offs)
+        nodes = held.tile([P, S], BF16, name="nodes")
+        nc.sync.dma_start(nodes[:], table)
+        weights = held.tile([P, M], BF16, name="weights")
+        nc.scalar.dma_start(weights[:], w)
+        bias = held.tile([P, BLOCKS], F32, name="bias")
+        with nc.allow_non_contiguous_dma(reason="one float32 bias value to a partition"):
+            nc.gpsimd.dma_start(bias[:], b.rearrange("(a p) o -> p (a o)", p=P))
+
+        pooled = held.tile([P, BLOCKS, V], F32, name="pooled")
+        for a in range(BLOCKS):
+            product = banks.tile([P, N], F32, name="product")
+            nc.tensor.matmul(
+                product[:],
+                weights[:, a * P : (a + 1) * P],
+                nodes[:].indirect(offsets[:]),
+                start=True,
+                stop=True,
+            )
+            squashed = work.tile([P, N], F32, name="squashed")
+            nc.scalar.activation(squashed[:], product[:], TANH, bias=bias[:, a : a + 1])
+            nc.vector.tensor_reduce(
+                pooled[:, a, :], squashed[:].rearrange("p (v t) -> p v t", t=D), axis=X, op=MAX
+            )
+        nc.sync.dma_start(out.rearrange("(a p) v -> p a v", p=P), pooled[:])

@@ -20,19 +20,26 @@ def tile_gather_matmul_kernel(tc, table, w, b, offs, out):
     nc = tc.nc
     with (
         tc.tile_pool(name="held", bufs=1) as held,
-        tc.tile_pool(name="work", bufs=2) as work,
         tc.psum_pool(name="banks", bufs=BLOCKS) as banks,
     ):
         offsets = held.tile([P, N // 16], U16, name="offsets")
         nc.sync.dma_start(offsets[:], offs)
         nodes = held.tile([P, S], BF16, name="nodes")
-        nc.sync.dma_start(nodes[:], table)
         weights = held.tile([P, M], BF16, name="weights")
-        nc.scalar.dma_start(weights[:], w)
         bias = held.tile([P, BLOCKS], F32, name="bias")
+        nc.scalar.dma_start(weights[:, 0:P], w[:, 0:P])
+        nc.sync.dma_start(nodes[:, 0 : S // 2], table[:, 0 : S // 2])
+        nc.scalar.dma_start(nodes[:, S // 2 : S], table[:, S // 2 : S])
+        nc.sync.dma_start(weights[:, P:M], w[:, P:M])
         with nc.allow_non_contiguous_dma(reason="one float32 bias value to a partition"):
-            nc.gpsimd.dma_start(bias[:], b.rearrange("(a p) o -> p (a o)", p=P))
+            nc.scalar.dma_start(bias[:], b.rearrange("(a p) o -> p (a o)", p=P))
 
+        zero = held.tile([P, 1], F32, name="zero")
+        nc.gpsimd.memset(zero[:], 0.0)
+        unused = held.tile([P, 1], F32, name="unused")
+        nc.scalar.activation(unused[:], zero[:], TANH)
+
+        largest = held.tile([P, BLOCKS, V], F32, name="largest")
         pooled = held.tile([P, BLOCKS, V], F32, name="pooled")
         for a in range(BLOCKS):
             product = banks.tile([P, N], F32, name="product")
@@ -43,9 +50,8 @@ def tile_gather_matmul_kernel(tc, table, w, b, offs, out):
                 start=True,
                 stop=True,
             )
-            squashed = work.tile([P, N], F32, name="squashed")
-            nc.scalar.activation(squashed[:], product[:], TANH, bias=bias[:, a : a + 1])
             nc.vector.tensor_reduce(
-                pooled[:, a, :], squashed[:].rearrange("p (v t) -> p v t", t=D), axis=X, op=MAX
+                largest[:, a, :], product[:].rearrange("p (v t) -> p v t", t=D), axis=X, op=MAX
             )
-        nc.sync.dma_start(out.rearrange("(a p) v -> p a v", p=P), pooled[:])
+            nc.scalar.activation(pooled[:, a, :], largest[:, a, :], TANH, bias=bias[:, a : a + 1])
+            nc.sync.dma_start(out[a * P : (a + 1) * P, :], pooled[:, a, :])

@@ -16,12 +16,20 @@ BLOCKS = M // P
 FLOPS = 2 * P * M * N
 
 
+WARM_MATMULS = 4
+REPEATS = 4
+
+
 def tile_gather_matmul_kernel(tc, table, w, b, offs, out):
     nc = tc.nc
     with (
         tc.tile_pool(name="held", bufs=1) as held,
         tc.psum_pool(name="banks", bufs=BLOCKS) as banks,
+        tc.psum_pool(name="idle", bufs=1) as idle,
     ):
+        zeros = held.tile([P, P], BF16, name="zeros")
+        nc.gpsimd.memset(zeros[:], 0.0)
+
         offsets = held.tile([P, N // 16], U16, name="offsets")
         nc.sync.dma_start(offsets[:], offs)
         nodes = held.tile([P, S], BF16, name="nodes")
@@ -34,10 +42,17 @@ def tile_gather_matmul_kernel(tc, table, w, b, offs, out):
         with nc.allow_non_contiguous_dma(reason="one float32 bias value to a partition"):
             nc.scalar.dma_start(bias[:], b.rearrange("(a p) o -> p (a o)", p=P))
 
-        zero = held.tile([P, 1], F32, name="zero")
-        nc.gpsimd.memset(zero[:], 0.0)
+        unread = idle.tile([P, REPEATS, P], F32, name="unread")
+        for i in range(WARM_MATMULS):
+            nc.tensor.matmul(
+                unread[:],
+                zeros[:],
+                zeros[:].unsqueeze(1).to_broadcast([P, REPEATS, P]),
+                start=True,
+                stop=True,
+            )
         unused = held.tile([P, 1], F32, name="unused")
-        nc.scalar.activation(unused[:], zero[:], TANH)
+        nc.scalar.activation(unused[:], zeros[:, 0:1], TANH)
 
         largest = held.tile([P, BLOCKS, V], F32, name="largest")
         pooled = held.tile([P, BLOCKS, V], F32, name="pooled")

@@ -16,43 +16,26 @@ BLOCKS = M // P
 FLOPS = 2 * P * M * N
 
 
-WARM_MATMULS = 4
-REPEATS = 4
-
-
 def tile_gather_matmul_kernel(tc, table, w, b, offs, out):
     nc = tc.nc
     with (
         tc.tile_pool(name="held", bufs=1) as held,
         tc.psum_pool(name="banks", bufs=BLOCKS) as banks,
-        tc.psum_pool(name="idle", bufs=1) as idle,
     ):
-        zeros = held.tile([P, P], BF16, name="zeros")
-        nc.gpsimd.memset(zeros[:], 0.0)
-
         offsets = held.tile([P, N // 16], U16, name="offsets")
         nc.sync.dma_start(offsets[:], offs)
         nodes = held.tile([P, S], BF16, name="nodes")
+        nc.sync.dma_start(nodes[:], table)
         weights = held.tile([P, M], BF16, name="weights")
+        nc.scalar.dma_start(weights[:], w)
         bias = held.tile([P, BLOCKS], F32, name="bias")
-        nc.scalar.dma_start(weights[:, 0:P], w[:, 0:P])
-        nc.sync.dma_start(nodes[:, 0 : S // 2], table[:, 0 : S // 2])
-        nc.scalar.dma_start(nodes[:, S // 2 : S], table[:, S // 2 : S])
-        nc.sync.dma_start(weights[:, P:M], w[:, P:M])
         with nc.allow_non_contiguous_dma(reason="one float32 bias value to a partition"):
             nc.scalar.dma_start(bias[:], b.rearrange("(a p) o -> p (a o)", p=P))
 
-        unread = idle.tile([P, REPEATS, P], F32, name="unread")
-        for i in range(WARM_MATMULS):
-            nc.tensor.matmul(
-                unread[:],
-                zeros[:],
-                zeros[:].unsqueeze(1).to_broadcast([P, REPEATS, P]),
-                start=True,
-                stop=True,
-            )
+        zero = held.tile([P, 1], F32, name="zero")
+        nc.gpsimd.memset(zero[:], 0.0)
         unused = held.tile([P, 1], F32, name="unused")
-        nc.scalar.activation(unused[:], zeros[:, 0:1], TANH)
+        nc.scalar.activation(unused[:], zero[:], TANH)
 
         largest = held.tile([P, BLOCKS, V], F32, name="largest")
         pooled = held.tile([P, BLOCKS, V], F32, name="pooled")

@@ -16,6 +16,10 @@ BLOCKS = M // P
 FLOPS = 2 * P * M * N
 
 
+SQUARE = 32
+QUADS = P // SQUARE
+
+
 def tile_gather_matmul_kernel(tc, table, w, b, offs, out):
     nc = tc.nc
     with (
@@ -28,9 +32,15 @@ def tile_gather_matmul_kernel(tc, table, w, b, offs, out):
         nc.sync.dma_start(nodes[:], table)
         weights = held.tile([P, M], BF16, name="weights")
         nc.scalar.dma_start(weights[:], w)
-        bias = held.tile([P, BLOCKS], F32, name="bias")
-        with nc.allow_non_contiguous_dma(reason="one float32 bias value to a partition"):
-            nc.scalar.dma_start(bias[:], b.rearrange("(a p) o -> p (a o)", p=P))
+
+        b_flat = held.tile([P, P], F32, name="b_flat", align_bytes=64)
+        nc.vector.memset(b_flat[:], 0.0)
+        nc.scalar.dma_start(
+            b_flat[0:P:SQUARE, :].rearrange("q (a r) -> q a r", r=SQUARE),
+            b.rearrange("(a q r) o -> q a (r o)", q=QUADS, r=SQUARE),
+        )
+        b_upright = held.tile([P, P], F32, name="b_upright", align_bytes=64)
+        nc.vector.transpose(b_upright[:], b_flat[:])
 
         zero = held.tile([P, 1], F32, name="zero")
         nc.gpsimd.memset(zero[:], 0.0)
@@ -51,5 +61,10 @@ def tile_gather_matmul_kernel(tc, table, w, b, offs, out):
             nc.vector.tensor_reduce(
                 largest[:, a, :], product[:].rearrange("p (v t) -> p v t", t=D), axis=X, op=MAX
             )
-            nc.scalar.activation(pooled[:, a, :], largest[:, a, :], TANH, bias=bias[:, a : a + 1])
+            nc.scalar.activation(
+                pooled[:, a, :],
+                largest[:, a, :],
+                TANH,
+                bias=b_upright[:, a * SQUARE : a * SQUARE + 1],
+            )
             nc.sync.dma_start(out[a * P : (a + 1) * P, :], pooled[:, a, :])

@@ -18,13 +18,14 @@ FLOPS = 2 * P * M * N
 
 SQUARE = 32
 QUADS = P // SQUARE
+CUT = 256
 
 
 def tile_gather_matmul_kernel(tc, table, w, b, offs, out):
     nc = tc.nc
     with (
         tc.tile_pool(name="held", bufs=1) as held,
-        tc.psum_pool(name="banks", bufs=BLOCKS) as banks,
+        tc.psum_pool(name="banks", bufs=BLOCKS + 1) as banks,
     ):
         offsets = held.tile([P, N // 16], U16, name="offsets")
         nc.sync.dma_start(offsets[:], offs)
@@ -49,22 +50,27 @@ def tile_gather_matmul_kernel(tc, table, w, b, offs, out):
 
         largest = held.tile([P, BLOCKS, V], F32, name="largest")
         pooled = held.tile([P, BLOCKS, V], F32, name="pooled")
-        for a in range(BLOCKS):
+        pieces = [(a, 0, N) for a in range(BLOCKS - 1)] + [(BLOCKS - 1, 0, CUT), (BLOCKS - 1, CUT, N)]
+        for a, first, end in pieces:
             product = banks.tile([P, N], F32, name="product")
             nc.tensor.matmul(
-                product[:],
+                product[:, 0 : end - first],
                 weights[:, a * P : (a + 1) * P],
-                nodes[:].indirect(offsets[:]),
+                nodes[:].indirect(offsets[:, first // 16 : end // 16]),
                 start=True,
                 stop=True,
             )
+            v0, v1 = first // D, end // D
             nc.vector.tensor_reduce(
-                largest[:, a, :], product[:].rearrange("p (v t) -> p v t", t=D), axis=X, op=MAX
+                largest[:, a, v0:v1],
+                product[:, 0 : end - first].rearrange("p (v t) -> p v t", t=D),
+                axis=X,
+                op=MAX,
             )
             nc.scalar.activation(
-                pooled[:, a, :],
-                largest[:, a, :],
+                pooled[:, a, v0:v1],
+                largest[:, a, v0:v1],
                 TANH,
                 bias=b_upright[:, a * SQUARE : a * SQUARE + 1],
             )
-            nc.sync.dma_start(out[a * P : (a + 1) * P, :], pooled[:, a, :])
+            nc.sync.dma_start(out[a * P : (a + 1) * P, v0:v1], pooled[:, a, v0:v1])

@@ -73,4 +73,5 @@ def tile_gather_matmul_kernel(tc, table, w, b, offs, out):
                 TANH,
                 bias=b_upright[:, a * SQUARE : a * SQUARE + 1],
             )
-            nc.sync.dma_start(out[a * P : (a + 1) * P, v0:v1], pooled[:, a, v0:v1])
+            if end == N:
+                nc.sync.dma_start(out[a * P : (a + 1) * P, :], pooled[:, a, :])

@@ -27,15 +27,17 @@ def tile_gather_matmul_kernel(tc, table, w, b, offs, out):
         tc.tile_pool(name="held", bufs=1) as held,
         tc.psum_pool(name="banks", bufs=BLOCKS + 1) as banks,
     ):
-        offsets = held.tile([P, N // 16], U16, name="offsets")
-        nc.sync.dma_start(offsets[:], offs)
         nodes = held.tile([P, S], BF16, name="nodes")
         nc.sync.dma_start(nodes[:], table)
+        offsets = held.tile([P, N // 16], U16, name="offsets")
+        nc.sync.dma_start(offsets[:], offs)
         weights = held.tile([P, M], BF16, name="weights")
         nc.scalar.dma_start(weights[:], w)
 
         b_flat = held.tile([P, P], F32, name="b_flat", align_bytes=64)
         nc.vector.memset(b_flat[:], 0.0)
+        zero = held.tile([P, 1], F32, name="zero")
+        nc.vector.memset(zero[:], 0.0)
         nc.scalar.dma_start(
             b_flat[0:P:SQUARE, :].rearrange("q (a r) -> q a r", r=SQUARE),
             b.rearrange("(a q r) o -> q a (r o)", q=QUADS, r=SQUARE),
@@ -43,8 +45,6 @@ def tile_gather_matmul_kernel(tc, table, w, b, offs, out):
         b_upright = held.tile([P, P], F32, name="b_upright", align_bytes=64)
         nc.vector.transpose(b_upright[:], b_flat[:])
 
-        zero = held.tile([P, 1], F32, name="zero")
-        nc.gpsimd.memset(zero[:], 0.0)
         unused = held.tile([P, 1], F32, name="unused")
         nc.scalar.activation(unused[:], zero[:], TANH)
 

@@ -32,7 +32,8 @@ def tile_gather_matmul_kernel(tc, table, w, b, offs, out):
         offsets = held.tile([P, N // 16], U16, name="offsets")
         nc.sync.dma_start(offsets[:], offs)
         weights = held.tile([P, M], BF16, name="weights")
-        nc.scalar.dma_start(weights[:], w)
+        nc.scalar.dma_start(weights[:, 0:P], w[:, 0:P])
+        nc.sync.dma_start(weights[:, P:M], w[:, P:M])
 
         b_flat = held.tile([P, P], F32, name="b_flat", align_bytes=64)
         nc.vector.memset(b_flat[:], 0.0)
@@ -73,5 +74,7 @@ def tile_gather_matmul_kernel(tc, table, w, b, offs, out):
                 TANH,
                 bias=b_upright[:, a * SQUARE : a * SQUARE + 1],
             )
-            if end == N:
+            if a == 1:
+                nc.sync.dma_start(out[0 : 2 * P, :].rearrange("(a p) v -> p a v", p=P), pooled[:, 0:2, :])
+            if a >= 2 and end == N:
                 nc.sync.dma_start(out[a * P : (a + 1) * P, :], pooled[:, a, :])

@@ -18,6 +18,7 @@ FLOPS = 2 * P * M * N
 
 SQUARE = 32
 QUADS = P // SQUARE
+HEAD = 128
 CUT = 256
 
 
@@ -25,7 +26,7 @@ def tile_gather_matmul_kernel(tc, table, w, b, offs, out):
     nc = tc.nc
     with (
         tc.tile_pool(name="held", bufs=1) as held,
-        tc.psum_pool(name="banks", bufs=BLOCKS + 1) as banks,
+        tc.psum_pool(name="banks", bufs=BLOCKS + 2) as banks,
     ):
         nodes = held.tile([P, S], BF16, name="nodes")
         nc.sync.dma_start(nodes[:], table)
@@ -51,7 +52,11 @@ def tile_gather_matmul_kernel(tc, table, w, b, offs, out):
 
         largest = held.tile([P, BLOCKS, V], F32, name="largest")
         pooled = held.tile([P, BLOCKS, V], F32, name="pooled")
-        pieces = [(a, 0, N) for a in range(BLOCKS - 1)] + [(BLOCKS - 1, 0, CUT), (BLOCKS - 1, CUT, N)]
+        pieces = (
+            [(0, 0, HEAD), (0, HEAD, N)]
+            + [(a, 0, N) for a in range(1, BLOCKS - 1)]
+            + [(BLOCKS - 1, 0, CUT), (BLOCKS - 1, CUT, N)]
+        )
         for a, first, end in pieces:
             product = banks.tile([P, N], F32, name="product")
             nc.tensor.matmul(

import concourse.mybir as mybir

BF16, F32, U16 = mybir.dt.bfloat16, mybir.dt.float32, mybir.dt.uint16
TANH = mybir.ActivationFunctionType.Tanh
MAX = mybir.AluOpType.max
X = mybir.AxisListType.X

P = 128
S = 1024
M = 512
N = 384
D = 4
V = N // D
BLOCKS = M // P

FLOPS = 2 * P * M * N


SQUARE = 32
QUADS = P // SQUARE
HEAD = 128
CUT = 256


def tile_gather_matmul_kernel(tc, table, w, b, offs, out):
    nc = tc.nc
    with (
        tc.tile_pool(name="held", bufs=1) as held,
        tc.psum_pool(name="banks", bufs=BLOCKS + 2) as banks,
    ):
        nodes = held.tile([P, S], BF16, name="nodes")
        nc.sync.dma_start(nodes[:], table)
        offsets = held.tile([P, N // 16], U16, name="offsets")
        nc.sync.dma_start(offsets[:], offs)
        weights = held.tile([P, M], BF16, name="weights")
        nc.scalar.dma_start(weights[:, 0:P], w[:, 0:P])
        nc.sync.dma_start(weights[:, P:M], w[:, P:M])

        b_flat = held.tile([P, P], F32, name="b_flat", align_bytes=64)
        nc.vector.memset(b_flat[:], 0.0)
        zero = held.tile([P, 1], F32, name="zero")
        nc.vector.memset(zero[:], 0.0)
        nc.scalar.dma_start(
            b_flat[0:P:SQUARE, :].rearrange("q (a r) -> q a r", r=SQUARE),
            b.rearrange("(a q r) o -> q a (r o)", q=QUADS, r=SQUARE),
        )
        b_upright = held.tile([P, P], F32, name="b_upright", align_bytes=64)
        nc.vector.transpose(b_upright[:], b_flat[:])

        unused = held.tile([P, 1], F32, name="unused")
        nc.scalar.activation(unused[:], zero[:], TANH)

        largest = held.tile([P, BLOCKS, V], F32, name="largest")
        pooled = held.tile([P, BLOCKS, V], F32, name="pooled")
        pieces = (
            [(0, 0, HEAD), (0, HEAD, N)]
            + [(a, 0, N) for a in range(1, BLOCKS - 1)]
            + [(BLOCKS - 1, 0, CUT), (BLOCKS - 1, CUT, N)]
        )
        for a, first, end in pieces:
            product = banks.tile([P, N], F32, name="product")
            nc.tensor.matmul(
                product[:, 0 : end - first],
                weights[:, a * P : (a + 1) * P],
                nodes[:].indirect(offsets[:, first // 16 : end // 16]),
                start=True,
                stop=True,
            )
            v0, v1 = first // D, end // D
            nc.vector.tensor_reduce(
                largest[:, a, v0:v1],
                product[:, 0 : end - first].rearrange("p (v t) -> p v t", t=D),
                axis=X,
                op=MAX,
            )
            nc.scalar.activation(
                pooled[:, a, v0:v1],
                largest[:, a, v0:v1],
                TANH,
                bias=b_upright[:, a * SQUARE : a * SQUARE + 1],
            )
            if a == 1:
                nc.sync.dma_start(out[0 : 2 * P, :].rearrange("(a p) v -> p a v", p=P), pooled[:, 0:2, :])
            if a >= 2 and end == N:
                nc.sync.dma_start(out[a * P : (a + 1) * P, :], pooled[:, a, :])
